import numpy as np
import ml_dtypes


def mxq(x, axis, fmt="e4m3"):
    dtype, down = {"e4m3": (ml_dtypes.float8_e4m3fn, 7), "e5m2": (ml_dtypes.float8_e5m2, 14)}[fmt]
    v = np.moveaxis(np.asarray(x, np.float32).astype(ml_dtypes.bfloat16).astype(np.float64), axis, -1)
    blocks = v.reshape(v.shape[:-1] + (-1, 32))
    amax = np.abs(blocks).max(-1, keepdims=True)
    byte = np.maximum(np.where(amax > 0, np.frexp(amax)[1] - 1 + 127, 0) - down, 1)
    scale = np.exp2(byte - 127.0)
    codes = (blocks / scale).astype(np.float32).astype(dtype).astype(np.float64)
    return np.moveaxis((codes * scale).reshape(v.shape), -1, axis)


WIDE = False


def mx_kscale(k):
    if not WIDE:
        return np.ones(k)
    levels = np.array([10, -10, 5, -5, 0])
    if k % 512:
        return np.exp2(np.random.permutation(np.resize(levels, k // 32))).repeat(32)
    a = np.empty((k // 512, 16))
    for p in range(k // 512):
        a[p, :8] = np.random.permutation(np.resize(levels, 8))
        for g in range(8):
            far = levels[np.abs(levels - a[p, g]) >= 10]
            a[p, g + 8] = far[np.random.randint(len(far))]
    return np.exp2(a.ravel()).repeat(32)


def f64(x):
    return np.asarray(x).astype(np.float64)


def striped(idx):
    return np.tile(idx.reshape(-1, 16).T, (8, 1)).astype(np.uint16)


def unstriped(offs):
    return offs[:16].T.reshape(-1).astype(np.int64)


E2M1 = np.array([0.0, 0.5, 1.0, 1.5, 2.0, 3.0, 4.0, 6.0, -0.0, -0.5, -1.0, -1.5, -2.0, -3.0, -4.0, -6.0])


def pack_weight(w, fmt):
    k, n = w.shape
    w = f64(np.asarray(w, np.float32).astype(ml_dtypes.bfloat16)).reshape(k // 32, 32, n)
    amax = np.abs(w).max(1)
    if fmt == "e4m3":
        byte = np.frexp(amax)[1] - 1 + 127 - 7
    else:
        mant, ex = np.frexp(amax / 6.0)
        byte = np.where(mant > 0.5, ex, ex - 1) + 127
    byte = np.clip(np.where(amax > 0, byte, 1), 1, 254)
    scaled = (w * np.exp2(127.0 - byte)[:, None, :]).reshape(k, n).astype(np.float32)
    by_word = np.ascontiguousarray(scaled.reshape(k // 512, 128, 4, n).transpose(0, 1, 3, 2))
    if fmt == "e4m3":
        words = by_word.astype(ml_dtypes.float8_e4m3fn).view(np.uint8)
    else:
        c = by_word.astype(ml_dtypes.float4_e2m1fn).view(np.uint8) & 0xF
        words = (c[..., 0::2] | (c[..., 1::2] << 4)).reshape(k // 512, 128, 2 * n)
    return np.ascontiguousarray(words), np.ascontiguousarray(byte.astype(np.uint8).reshape(k // 512, 16, n))


def unpack_weight(words, scales, fmt):
    g, _, n = scales.shape
    words = np.ascontiguousarray(words).reshape(g, 128, n, -1)
    if fmt == "e4m3":
        vals = words.view(ml_dtypes.float8_e4m3fn).astype(np.float64)
    else:
        nib = np.empty((g, 128, n, 4), np.uint8)
        nib[..., 0::2] = words & 0xF
        nib[..., 1::2] = words >> 4
        vals = E2M1[nib]
    vals = vals * np.repeat(np.exp2(scales.astype(np.float64) - 127.0), 8, axis=1)[..., None]
    return vals.transpose(0, 1, 3, 2).reshape(g * 512, n)


def sigmoid(v):
    return 1.0 / (1.0 + np.exp(-np.maximum(v, -700.0)))


K, T, E, C, H, N = 512, 512, 8, 128, 512, 384


def by_expert(wq, xq):
    return np.concatenate([wq[e].T @ xq[:, e * C:(e + 1) * C] for e in range(E)], axis=1)


def setup_inputs():
    n = np.random.standard_normal
    s = mx_kscale(K)[:, None]
    u = mx_kscale(H)
    first = np.random.permutation(np.repeat(np.arange(E), T // E))
    second = (first + 1 + np.random.permutation(np.repeat(np.arange(E - 1), -(-T // (E - 1)))[:T])) % E
    while np.bincount(second, minlength=E).max() != T // E:
        load = np.bincount(second, minlength=E); hi, lo = int(load.argmax()), int(load.argmin())
        t = np.flatnonzero((second == hi) & (first != lo))[0]; second[t] = lo
    slot_token = np.empty(E * C, np.int64); pos = np.empty((2, T), np.int64); fill = np.zeros(E, np.int64)
    place = np.stack([np.random.permutation(C) for _ in range(E)])
    for r, deal in enumerate((first, second)):
        for t in np.random.permutation(T):
            e = deal[t]; j = e * C + place[e, fill[e]]; fill[e] += 1; slot_token[j] = t; pos[r, t] = j
    g = np.random.uniform(0.2, 0.8, T)
    w1 = [pack_weight(m, "e2m1") for m in n((E, K, H)) / np.sqrt(K) / s[None]]
    w3 = [pack_weight(m, "e2m1") for m in n((E, K, H)) / np.sqrt(K) / s[None] * u[None, None, :]]
    w2 = [pack_weight(m, "e2m1") for m in n((E, H, N)) / np.sqrt(H) / u[None, :, None]]
    return {
        "xT": (n((K, T)) * s).astype(np.float32),
        "w1_words": np.stack([m[0] for m in w1]),
        "w1_scales": np.stack([m[1] for m in w1]),
        "w3_words": np.stack([m[0] for m in w3]),
        "w3_scales": np.stack([m[1] for m in w3]),
        "w2_words": np.stack([m[0] for m in w2]),
        "w2_scales": np.stack([m[1] for m in w2]),
        "gate": np.stack([np.tile(g, (N, 1)), np.tile(1.0 - g, (N, 1))]).astype(np.float32),
        "offs": striped(slot_token),
        "pos1": striped(pos[0]),
        "pos2": striped(pos[1]),
    }


def reference(xT, w1_words, w1_scales, w3_words, w3_scales, w2_words, w2_scales, gate, offs, pos1, pos2):
    idx = unstriped(offs)
    w1 = np.stack([unpack_weight(w1_words[e], w1_scales[e], "e2m1") for e in range(E)])
    w3 = np.stack([unpack_weight(w3_words[e], w3_scales[e], "e2m1") for e in range(E)])
    w2 = np.stack([unpack_weight(w2_words[e], w2_scales[e], "e2m1") for e in range(E)])
    xq = mxq(f64(xT)[:, idx], 0, "e4m3")
    h = sigmoid(by_expert(w1, xq))
    h = h * by_expert(w3, xq)
    y = by_expert(w2, mxq(h, 0, "e4m3"))
    return f64(gate[0]) * y[:, unstriped(pos1)] + f64(gate[1]) * y[:, unstriped(pos2)]

@@ -1,0 +1,209 @@
+from contextlib import ExitStack
+
+import concourse.mybir as mybir
+from concourse.masks import make_identity
+
+P = 128
+T, E, C, K, H, N = 512, 8, 128, 512, 512, 384
+NT = N // P
+HALF = T // 2
+FLOPS = 2 * E * C * (2 * K * H + H * N)
+
+F32 = mybir.dt.float32
+BF16 = mybir.dt.bfloat16
+I32 = mybir.dt.int32
+U32 = mybir.dt.uint32
+U16 = mybir.dt.uint16
+U8 = mybir.dt.uint8
+FP8X4 = mybir.dt.float8_e4m3fn_x4
+FP4X4 = mybir.dt.float4_e2m1fn_x4
+MULT = mybir.AluOpType.mult
+ADD = mybir.AluOpType.add
+SIGMOID = mybir.ActivationFunctionType.Sigmoid
+
+WEIGHT_GROUPS = ((0, 2), (2, 5), (5, 8))
+VEC_COLS = 176
+Y_ON_VECTOR = {5: 1, 6: 1, 7: 2}
+
+
+def tile_moe_pln_glu_sigmoid_kernel(
+    tc, xT, w1_words, w1_scales, w3_words, w3_scales, w2_words, w2_scales, gate, offs, pos1, pos2, out
+):
+    nc = tc.nc
+    with ExitStack() as ctx:
+        keep = ctx.enter_context(tc.tile_pool(name="keep", bufs=1))
+        work = ctx.enter_context(tc.tile_pool(name="work", bufs=3))
+        psum = ctx.enter_context(tc.psum_pool(name="psum", bufs=2))
+
+        offs_sb = keep.tile([P, E * C // 16], U16, name="offs_sb")
+        pos1_sb = keep.tile([P, T // 16], U16, name="pos1_sb")
+        pos2_sb = keep.tile([P, T // 16], U16, name="pos2_sb")
+
+        x_raw = [keep.tile([P, 4, HALF], F32, name=f"x_raw{h}") for h in range(2)]
+        x_grp = [keep.tile([P, HALF, 4], BF16, name=f"x_grp{h}", align_bytes=64) for h in range(2)]
+        x_words = keep.tile([P, T], U32, name="x_words", align_bytes=64)
+        x_bytes = keep.tile([P, T], U8, name="x_bytes", align_bytes=64)
+        xv = xT.rearrange("(p j) t -> p j t", j=4)
+        for h in range(2):
+            nc.sync.dma_start(out=x_raw[h][:], in_=xv[:, :, h * HALF : (h + 1) * HALF])
+        nc.sync.dma_start(offs_sb[:], offs)
+
+        w1_sc = keep.tile([P, E * H], U8, name="w1_sc", align_bytes=64)
+        w3_sc = keep.tile([P, E * H], U8, name="w3_sc", align_bytes=64)
+        w2_sc = keep.tile([P, E * N], U8, name="w2_sc", align_bytes=64)
+        warm = keep.tile([P, 1], F32, name="warm")
+        nc.vector.memset(warm[:], 0.0)
+        nc.scalar.activation(warm[:], warm[:], SIGMOID)
+        nc.vector.memset(w1_sc[:].bitcast(I32), 0)
+        nc.vector.memset(w3_sc[:].bitcast(I32), 0)
+        nc.vector.memset(x_bytes[:].bitcast(I32), 0)
+        nc.vector.memset(w2_sc[:].bitcast(I32), 0)
+
+        def load_scales(queue, sc, src):
+            for q in range(4):
+                queue.dma_start(
+                    out=sc[32 * q : 32 * q + 4, :].bitcast(I32).rearrange("p (e n) -> p e n", e=E),
+                    in_=src[:, 0, 4 * q : 4 * q + 4, :].rearrange("e q n -> q e n").bitcast(I32),
+                )
+
+        ident = keep.tile([P, P], F32, name="ident")
+        make_identity(nc, ident[:])
+        load_scales(nc.scalar, w1_sc, w1_scales)
+        load_scales(nc.scalar, w3_sc, w3_scales)
+        load_scales(nc.gpsimd, w2_sc, w2_scales)
+
+        w1_sb, w3_sb, w2_sb = {}, {}, {}
+        for lo, hi in WEIGHT_GROUPS:
+            n_e = hi - lo
+            for held, words, label in ((w1_sb, w1_words, "w1"), (w3_sb, w3_words, "w3"), (w2_sb, w2_words, "w2")):
+                width = words.shape[3]
+                tile = keep.tile([P, n_e * width], U8, name=f"{label}_{lo}", align_bytes=64)
+                nc.sync.dma_start(
+                    out=tile[:].bitcast(I32).rearrange("p (e n) -> p e n", e=n_e),
+                    in_=words[lo:hi, 0].rearrange("e p n -> p e n").bitcast(I32),
+                )
+                for e in range(lo, hi):
+                    held[e] = tile[:, (e - lo) * width : (e - lo + 1) * width]
+        nc.sync.dma_start(pos1_sb[:], pos1)
+        nc.sync.dma_start(pos2_sb[:], pos2)
+        gates = []
+        for g in range(2):
+            gt = keep.tile([P, NT, T], F32, name=f"gate{g}")
+            nc.sync.dma_start(out=gt[:], in_=gate[g].rearrange("(a p) t -> p a t", p=P))
+            gates.append(gt)
+
+        for h in range(2):
+            dst = x_grp[h]
+            src = x_raw[h][:].rearrange("p j t -> p t j")
+            nc.vector.tensor_copy(out=dst[:, :VEC_COLS, :], in_=src[:, :VEC_COLS, :])
+            nc.scalar.copy(out=dst[:, VEC_COLS:, :], in_=src[:, VEC_COLS:, :])
+        for h in range(2):
+            cols = slice(h * HALF, (h + 1) * HALF)
+            nc.vector.quantize_mx(
+                out=x_words[:, cols].bitcast(FP8X4),
+                scales=x_bytes[:, cols],
+                in_=x_grp[h][:].rearrange("p t j -> p (t j)"),
+            )
+
+        tok_words, tok_bytes = {}, {}
+
+        def gather(lo, hi):
+            width = (hi - lo) * C
+            gw = keep.tile([P, width], U32, name=f"gw_{lo}", align_bytes=64)
+            gb = keep.tile([P, width], U8, name=f"gb_{lo}", align_bytes=64)
+            part = offs_sb[:, lo * C // 16 : hi * C // 16]
+            nc.vector.tensor_copy(gw[:], x_words[:].indirect(part))
+            nc.vector.tensor_copy(gb[:], x_bytes[:].indirect(part))
+            for e in range(lo, hi):
+                tok_words[e] = gw[:, (e - lo) * C : (e - lo + 1) * C]
+                tok_bytes[e] = gb[:, (e - lo) * C : (e - lo + 1) * C]
+
+        y_sb = [keep.tile([P, E * C], F32, name=f"y_sb{n}") for n in range(NT)]
+        live = {}
+
+        def first_layer(e):
+            a_ps = psum.tile([C, H], F32, name="a_ps")
+            g_ps = psum.tile([C, H], F32, name="g_ps")
+            for ps, held, sc in ((a_ps, w1_sb, w1_sc), (g_ps, w3_sb, w3_sc)):
+                nc.tensor.matmul_mx(
+                    out=ps[:],
+                    lhsT=tok_words[e].bitcast(FP8X4),
+                    lhsT_scale=tok_bytes[e],
+                    rhs=held[e].bitcast(FP4X4),
+                    rhs_scale=sc[:, e * H : (e + 1) * H],
+                    start=True,
+                    stop=True,
+                )
+            sig = work.tile([C, H], F32, name="sig")
+            nc.scalar.activation(sig[:], a_ps[:], SIGMOID)
+            live[e] = (sig, g_ps)
+
+        def product(e):
+            sig, g_ps = live[e]
+            h_row = work.tile([C, H], BF16, name="h_row", align_bytes=64)
+            nc.vector.tensor_tensor(h_row[:], sig[:], g_ps[:], MULT)
+            live[e] = h_row
+
+        def turn_h(e):
+            h_pairs = live[e][:].bitcast(F32)
+            turn = psum.tile([P, 2, C], F32, name="turn")
+            for u in range(2):
+                nc.tensor.transpose(turn[:, u, :], h_pairs[:, u : H // 2 : 2], ident[:])
+            h_grp = work.tile([P, C * 4], BF16, name="h_grp", align_bytes=64)
+            nc.scalar.copy(
+                out=h_grp[:].bitcast(F32).rearrange("p (c u) -> p c u", u=2),
+                in_=turn[:].rearrange("p u c -> p c u"),
+            )
+            live[e] = h_grp
+
+        def quantise_h(e):
+            h_words = work.tile([P, C], U32, name="h_words", align_bytes=64)
+            h_bytes = work.tile([P, C], U8, name="h_bytes", align_bytes=64)
+            nc.vector.quantize_mx(out=h_words[:].bitcast(FP8X4), scales=h_bytes[:], in_=live[e][:])
+            live[e] = (h_words, h_bytes)
+
+        def second_layer(e):
+            h_words, h_bytes = live[e]
+            y_ps = psum.tile([P, N], F32, name="y_ps")
+            for n in range(NT):
+                nc.tensor.matmul_mx(
+                    out=y_ps[:, n * P : (n + 1) * P],
+                    lhsT=w2_sb[e][:, 2 * P * n : 2 * P * (n + 1)].bitcast(FP4X4),
+                    lhsT_scale=w2_sc[:, e * N + n * P : e * N + (n + 1) * P],
+                    rhs=h_words[:].bitcast(FP8X4),
+                    rhs_scale=h_bytes[:],
+                    start=True,
+                    stop=True,
+                )
+            live[e] = y_ps
+
+        def keep_y(e):
+            for n in range(NT):
+                copy = nc.vector.tensor_copy if n < Y_ON_VECTOR.get(e, 0) else nc.scalar.copy
+                copy(out=y_sb[n][:, e * C : (e + 1) * C], in_=live[e][:, n * P : (n + 1) * P])
+
+        gathers = {-2: ((0, 1), (1, 2)), 0: ((2, 4),), 2: ((4, 6),), 4: ((6, 8),)}
+        for s in range(-2, E + 3):
+            for lo, hi in gathers.get(s, ()):
+                gather(lo, hi)
+            if 0 <= s < E:
+                product(s)
+            if 0 <= s - 2 < E:
+                quantise_h(s - 2)
+            if 0 <= s - 3 < E:
+                keep_y(s - 3)
+            if 0 <= s + 2 < E:
+                first_layer(s + 2)
+            if 0 <= s < E:
+                turn_h(s)
+            if 0 <= s - 2 < E:
+                second_layer(s - 2)
+
+        for n in range(NT):
+            first = work.tile([P, T], F32, name="first")
+            second = work.tile([P, T], F32, name="second")
+            result = work.tile([P, T], F32, name="result")
+            nc.vector.tensor_tensor(first[:], y_sb[n][:].indirect(pos1_sb[:]), gates[0][:, n, :], MULT)
+            nc.vector.tensor_tensor(second[:], y_sb[n][:].indirect(pos2_sb[:]), gates[1][:, n, :], MULT)
+            nc.vector.tensor_tensor(result[:], first[:], second[:], ADD)
+            nc.sync.dma_start(out=out[n * P : (n + 1) * P, :], in_=result[:])

@@ -21,7 +21,6 @@ MULT = mybir.AluOpType.mult
 ADD = mybir.AluOpType.add
 SIGMOID = mybir.ActivationFunctionType.Sigmoid
 
-WEIGHT_GROUPS = ((0, 2), (2, 5), (5, 8))
 VEC_COLS = 176
 Y_ON_VECTOR = {5: 1, 6: 1, 7: 2}
 
@@ -48,42 +47,52 @@ def tile_moe_pln_glu_sigmoid_kernel(
             nc.sync.dma_start(out=x_raw[h][:], in_=xv[:, :, h * HALF : (h + 1) * HALF])
         nc.sync.dma_start(offs_sb[:], offs)
 
-        w1_sc = keep.tile([P, E * H], U8, name="w1_sc", align_bytes=64)
-        w3_sc = keep.tile([P, E * H], U8, name="w3_sc", align_bytes=64)
-        w2_sc = keep.tile([P, E * N], U8, name="w2_sc", align_bytes=64)
-        warm = keep.tile([P, 1], F32, name="warm")
-        nc.vector.memset(warm[:], 0.0)
-        nc.scalar.activation(warm[:], warm[:], SIGMOID)
-        nc.vector.memset(w1_sc[:].bitcast(I32), 0)
-        nc.vector.memset(w3_sc[:].bitcast(I32), 0)
-        nc.vector.memset(x_bytes[:].bitcast(I32), 0)
-        nc.vector.memset(w2_sc[:].bitcast(I32), 0)
-
-        def load_scales(queue, sc, src):
-            for q in range(4):
+        def load_scales(queue, plane, src, quadrants):
+            for q in quadrants:
                 queue.dma_start(
-                    out=sc[32 * q : 32 * q + 4, :].bitcast(I32).rearrange("p (e n) -> p e n", e=E),
+                    out=plane[32 * q : 32 * q + 4, :].bitcast(I32).rearrange("p (e n) -> p e n", e=E),
                     in_=src[:, 0, 4 * q : 4 * q + 4, :].rearrange("e q n -> q e n").bitcast(I32),
                 )
 
+        planes = {}
+        for label, width in (("w1", H), ("w3", H), ("w2", N)):
+            planes[label] = keep.tile([P, E * width], U8, name=f"{label}_sc", align_bytes=64)
+        warm = keep.tile([P, 1], F32, name="warm")
+        nc.vector.memset(warm[:], 0.0)
+        nc.scalar.activation(warm[:], warm[:], SIGMOID)
+        nc.vector.memset(planes["w1"][:].bitcast(I32), 0)
+        nc.vector.memset(planes["w3"][:].bitcast(I32), 0)
+        nc.vector.memset(x_bytes[:].bitcast(I32), 0)
+        nc.vector.memset(planes["w2"][:].bitcast(I32), 0)
         ident = keep.tile([P, P], F32, name="ident")
         make_identity(nc, ident[:])
-        load_scales(nc.scalar, w1_sc, w1_scales)
-        load_scales(nc.scalar, w3_sc, w3_scales)
-        load_scales(nc.gpsimd, w2_sc, w2_scales)
 
-        w1_sb, w3_sb, w2_sb = {}, {}, {}
-        for lo, hi in WEIGHT_GROUPS:
-            n_e = hi - lo
-            for held, words, label in ((w1_sb, w1_words, "w1"), (w3_sb, w3_words, "w3"), (w2_sb, w2_words, "w2")):
-                width = words.shape[3]
-                tile = keep.tile([P, n_e * width], U8, name=f"{label}_{lo}", align_bytes=64)
-                nc.sync.dma_start(
-                    out=tile[:].bitcast(I32).rearrange("p (e n) -> p e n", e=n_e),
-                    in_=words[lo:hi, 0].rearrange("e p n -> p e n").bitcast(I32),
-                )
-                for e in range(lo, hi):
-                    held[e] = tile[:, (e - lo) * width : (e - lo + 1) * width]
+        words_of = {}
+
+        def load_words(label, words, lo, hi):
+            width = words.shape[3]
+            tile = keep.tile([P, (hi - lo) * width], U8, name=f"{label}_{lo}", align_bytes=64)
+            nc.sync.dma_start(
+                out=tile[:].bitcast(I32).rearrange("p (e n) -> p e n", e=hi - lo),
+                in_=words[lo:hi, 0].rearrange("e p n -> p e n").bitcast(I32),
+            )
+            for e in range(lo, hi):
+                words_of[label, e] = tile[:, (e - lo) * width : (e - lo + 1) * width]
+
+        load_words("w1", w1_words, 0, 2)
+        load_words("w3", w3_words, 0, 2)
+        load_scales(nc.sync, planes["w1"], w1_scales, range(4))
+        load_scales(nc.gpsimd, planes["w3"], w3_scales, (3,))
+        load_scales(nc.sync, planes["w3"], w3_scales, range(3))
+        load_words("w1", w1_words, 2, 4)
+        load_words("w3", w3_words, 2, 4)
+        load_words("w2", w2_words, 0, 2)
+        load_scales(nc.sync, planes["w2"], w2_scales, range(4))
+        load_words("w2", w2_words, 2, 4)
+        for lo in (4, 6):
+            load_words("w1", w1_words, lo, lo + 2)
+            load_words("w3", w3_words, lo, lo + 2)
+            load_words("w2", w2_words, lo, lo + 2)
         nc.sync.dma_start(pos1_sb[:], pos1)
         nc.sync.dma_start(pos2_sb[:], pos2)
         gates = []
@@ -124,13 +133,13 @@ def tile_moe_pln_glu_sigmoid_kernel(
         def first_layer(e):
             a_ps = psum.tile([C, H], F32, name="a_ps")
             g_ps = psum.tile([C, H], F32, name="g_ps")
-            for ps, held, sc in ((a_ps, w1_sb, w1_sc), (g_ps, w3_sb, w3_sc)):
+            for ps, label in ((a_ps, "w1"), (g_ps, "w3")):
                 nc.tensor.matmul_mx(
                     out=ps[:],
                     lhsT=tok_words[e].bitcast(FP8X4),
                     lhsT_scale=tok_bytes[e],
-                    rhs=held[e].bitcast(FP4X4),
-                    rhs_scale=sc[:, e * H : (e + 1) * H],
+                    rhs=words_of[label, e].bitcast(FP4X4),
+                    rhs_scale=planes[label][:, e * H : (e + 1) * H],
                     start=True,
                     stop=True,
                 )
@@ -168,8 +177,8 @@ def tile_moe_pln_glu_sigmoid_kernel(
             for n in range(NT):
                 nc.tensor.matmul_mx(
                     out=y_ps[:, n * P : (n + 1) * P],
-                    lhsT=w2_sb[e][:, 2 * P * n : 2 * P * (n + 1)].bitcast(FP4X4),
-                    lhsT_scale=w2_sc[:, e * N + n * P : e * N + (n + 1) * P],
+                    lhsT=words_of["w2", e][:, 2 * P * n : 2 * P * (n + 1)].bitcast(FP4X4),
+                    lhsT_scale=planes["w2"][:, e * N + n * P : e * N + (n + 1) * P],
                     rhs=h_words[:].bitcast(FP8X4),
                     rhs_scale=h_bytes[:],
                     start=True,
@@ -205,5 +214,8 @@ def tile_moe_pln_glu_sigmoid_kernel(
             result = work.tile([P, T], F32, name="result")
             nc.vector.tensor_tensor(first[:], y_sb[n][:].indirect(pos1_sb[:]), gates[0][:, n, :], MULT)
             nc.vector.tensor_tensor(second[:], y_sb[n][:].indirect(pos2_sb[:]), gates[1][:, n, :], MULT)
-            nc.vector.tensor_tensor(result[:], first[:], second[:], ADD)
-            nc.sync.dma_start(out=out[n * P : (n + 1) * P, :], in_=result[:])
+            pieces = 2 if n == NT - 1 else 1
+            for i in range(pieces):
+                cols = slice(i * T // pieces, (i + 1) * T // pieces)
+                nc.vector.tensor_tensor(result[:, cols], first[:, cols], second[:, cols], ADD)
+                nc.sync.dma_start(out=out[n * P : (n + 1) * P, cols], in_=result[:, cols])

@@ -47,11 +47,11 @@ def tile_moe_pln_glu_sigmoid_kernel(
             nc.sync.dma_start(out=x_raw[h][:], in_=xv[:, :, h * HALF : (h + 1) * HALF])
         nc.sync.dma_start(offs_sb[:], offs)
 
-        def load_scales(queue, plane, src, quadrants):
-            for q in quadrants:
-                queue.dma_start(
-                    out=plane[32 * q : 32 * q + 4, :].bitcast(I32).rearrange("p (e n) -> p e n", e=E),
-                    in_=src[:, 0, 4 * q : 4 * q + 4, :].rearrange("e q n -> q e n").bitcast(I32),
+        def load_scales(plane, src):
+            for r in range(4):
+                nc.sync.dma_start(
+                    out=plane[r:P:32, :].bitcast(I32).rearrange("q (e n) -> q e n", e=E),
+                    in_=src[:, 0, r:16:4, :].rearrange("e q n -> q e n").bitcast(I32),
                 )
 
         planes = {}
@@ -81,13 +81,12 @@ def tile_moe_pln_glu_sigmoid_kernel(
 
         load_words("w1", w1_words, 0, 2)
         load_words("w3", w3_words, 0, 2)
-        load_scales(nc.sync, planes["w1"], w1_scales, range(4))
-        load_scales(nc.gpsimd, planes["w3"], w3_scales, (3,))
-        load_scales(nc.sync, planes["w3"], w3_scales, range(3))
+        load_scales(planes["w1"], w1_scales)
+        load_scales(planes["w3"], w3_scales)
         load_words("w1", w1_words, 2, 4)
         load_words("w3", w3_words, 2, 4)
         load_words("w2", w2_words, 0, 2)
-        load_scales(nc.sync, planes["w2"], w2_scales, range(4))
+        load_scales(planes["w2"], w2_scales)
         load_words("w2", w2_words, 2, 4)
         for lo in (4, 6):
             load_words("w1", w1_words, lo, lo + 2)
@@ -150,14 +149,19 @@ def tile_moe_pln_glu_sigmoid_kernel(
         def product(e):
             sig, g_ps = live[e]
             h_row = work.tile([C, H], BF16, name="h_row", align_bytes=64)
-            nc.vector.tensor_tensor(h_row[:], sig[:], g_ps[:], MULT)
+            nc.vector.tensor_tensor(
+                h_row[:].rearrange("c (u m d) -> c u m d", u=2, d=2),
+                sig[:].rearrange("c (m u d) -> c u m d", u=2, d=2),
+                g_ps[:].rearrange("c (m u d) -> c u m d", u=2, d=2),
+                MULT,
+            )
             live[e] = h_row
 
         def turn_h(e):
             h_pairs = live[e][:].bitcast(F32)
             turn = psum.tile([P, 2, C], F32, name="turn")
             for u in range(2):
-                nc.tensor.transpose(turn[:, u, :], h_pairs[:, u : H // 2 : 2], ident[:])
+                nc.tensor.transpose(turn[:, u, :], h_pairs[:, u * P : (u + 1) * P], ident[:])
             h_grp = work.tile([P, C * 4], BF16, name="h_grp", align_bytes=64)
             nc.scalar.copy(
                 out=h_grp[:].bitcast(F32).rearrange("p (c u) -> p c u", u=2),

@@ -21,7 +21,7 @@ MULT = mybir.AluOpType.mult
 ADD = mybir.AluOpType.add
 SIGMOID = mybir.ActivationFunctionType.Sigmoid
 
-VEC_COLS = 176
+X_CHUNKS = ((0, 256), (256, 384), (384, 512))
 Y_ON_VECTOR = {5: 1, 6: 1, 7: 2}
 
 
@@ -38,13 +38,13 @@ def tile_moe_pln_glu_sigmoid_kernel(
         pos1_sb = keep.tile([P, T // 16], U16, name="pos1_sb")
         pos2_sb = keep.tile([P, T // 16], U16, name="pos2_sb")
 
-        x_raw = [keep.tile([P, 4, HALF], F32, name=f"x_raw{h}") for h in range(2)]
-        x_grp = [keep.tile([P, HALF, 4], BF16, name=f"x_grp{h}", align_bytes=64) for h in range(2)]
+        x_raw = [keep.tile([P, 4, hi - lo], F32, name=f"x_raw{lo}") for lo, hi in X_CHUNKS]
+        x_grp = [keep.tile([P, hi - lo, 4], BF16, name=f"x_grp{lo}", align_bytes=64) for lo, hi in X_CHUNKS]
         x_words = keep.tile([P, T], U32, name="x_words", align_bytes=64)
         x_bytes = keep.tile([P, T], U8, name="x_bytes", align_bytes=64)
         xv = xT.rearrange("(p j) t -> p j t", j=4)
-        for h in range(2):
-            nc.sync.dma_start(out=x_raw[h][:], in_=xv[:, :, h * HALF : (h + 1) * HALF])
+        for i, (lo, hi) in enumerate(X_CHUNKS):
+            nc.sync.dma_start(out=x_raw[i][:], in_=xv[:, :, lo:hi])
         nc.sync.dma_start(offs_sb[:], offs)
 
         def load_scales(plane, src):
@@ -60,10 +60,10 @@ def tile_moe_pln_glu_sigmoid_kernel(
         warm = keep.tile([P, 1], F32, name="warm")
         nc.vector.memset(warm[:], 0.0)
         nc.scalar.activation(warm[:], warm[:], SIGMOID)
-        nc.vector.memset(planes["w1"][:].bitcast(I32), 0)
+        nc.gpsimd.memset(planes["w1"][:].bitcast(I32), 0)
         nc.vector.memset(planes["w3"][:].bitcast(I32), 0)
-        nc.vector.memset(x_bytes[:].bitcast(I32), 0)
         nc.vector.memset(planes["w2"][:].bitcast(I32), 0)
+        nc.vector.memset(x_bytes[:].bitcast(I32), 0)
         ident = keep.tile([P, P], F32, name="ident")
         make_identity(nc, ident[:])
 
@@ -79,19 +79,17 @@ def tile_moe_pln_glu_sigmoid_kernel(
             for e in range(lo, hi):
                 words_of[label, e] = tile[:, (e - lo) * width : (e - lo + 1) * width]
 
+        load_scales(planes["w1"], w1_scales)
         load_words("w1", w1_words, 0, 2)
         load_words("w3", w3_words, 0, 2)
-        load_scales(planes["w1"], w1_scales)
         load_scales(planes["w3"], w3_scales)
-        load_words("w1", w1_words, 2, 4)
-        load_words("w3", w3_words, 2, 4)
-        load_words("w2", w2_words, 0, 2)
+        load_words("w1", w1_words, 2, 5)
+        load_words("w3", w3_words, 2, 5)
+        load_words("w2", w2_words, 0, 3)
         load_scales(planes["w2"], w2_scales)
-        load_words("w2", w2_words, 2, 4)
-        for lo in (4, 6):
-            load_words("w1", w1_words, lo, lo + 2)
-            load_words("w3", w3_words, lo, lo + 2)
-            load_words("w2", w2_words, lo, lo + 2)
+        load_words("w1", w1_words, 5, 8)
+        load_words("w3", w3_words, 5, 8)
+        load_words("w2", w2_words, 3, 8)
         nc.sync.dma_start(pos1_sb[:], pos1)
         nc.sync.dma_start(pos2_sb[:], pos2)
         gates = []
@@ -100,17 +98,15 @@ def tile_moe_pln_glu_sigmoid_kernel(
             nc.sync.dma_start(out=gt[:], in_=gate[g].rearrange("(a p) t -> p a t", p=P))
             gates.append(gt)
 
-        for h in range(2):
-            dst = x_grp[h]
-            src = x_raw[h][:].rearrange("p j t -> p t j")
-            nc.vector.tensor_copy(out=dst[:, :VEC_COLS, :], in_=src[:, :VEC_COLS, :])
-            nc.scalar.copy(out=dst[:, VEC_COLS:, :], in_=src[:, VEC_COLS:, :])
-        for h in range(2):
-            cols = slice(h * HALF, (h + 1) * HALF)
+        for i, (lo, hi) in enumerate(X_CHUNKS):
+            src = x_raw[i][:].rearrange("p j t -> p t j")
+            split = (hi - lo) * 11 // 16
+            nc.vector.tensor_copy(out=x_grp[i][:, :split, :], in_=src[:, :split, :])
+            nc.scalar.copy(out=x_grp[i][:, split:, :], in_=src[:, split:, :])
             nc.vector.quantize_mx(
-                out=x_words[:, cols].bitcast(FP8X4),
-                scales=x_bytes[:, cols],
-                in_=x_grp[h][:].rearrange("p t j -> p (t j)"),
+                out=x_words[:, lo:hi].bitcast(FP8X4),
+                scales=x_bytes[:, lo:hi],
+                in_=x_grp[i][:].rearrange("p t j -> p (t j)"),
             )
 
         tok_words, tok_bytes = {}, {}
@@ -212,14 +208,29 @@ def tile_moe_pln_glu_sigmoid_kernel(
             if 0 <= s - 2 < E:
                 second_layer(s - 2)
 
-        for n in range(NT):
-            first = work.tile([P, T], F32, name="first")
-            second = work.tile([P, T], F32, name="second")
-            result = work.tile([P, T], F32, name="result")
-            nc.vector.tensor_tensor(first[:], y_sb[n][:].indirect(pos1_sb[:]), gates[0][:, n, :], MULT)
-            nc.vector.tensor_tensor(second[:], y_sb[n][:].indirect(pos2_sb[:]), gates[1][:, n, :], MULT)
-            pieces = 2 if n == NT - 1 else 1
-            for i in range(pieces):
-                cols = slice(i * T // pieces, (i + 1) * T // pieces)
-                nc.vector.tensor_tensor(result[:, cols], first[:, cols], second[:, cols], ADD)
-                nc.sync.dma_start(out=out[n * P : (n + 1) * P, cols], in_=result[:, cols])
+        parts = {}
+
+        def pick(n, which, lo, hi):
+            if (n, which) not in parts:
+                parts[n, which] = keep.tile([P, T], F32, name=f"part{n}{which}")
+            pos = (pos1_sb, pos2_sb)[which]
+            nc.vector.tensor_tensor(
+                parts[n, which][:, lo:hi], y_sb[n][:].indirect(pos[:, lo // 16 : hi // 16]), gates[which][:, n, lo:hi], MULT
+            )
+
+        def store(n, lo, hi):
+            result = work.tile([P, hi - lo], F32, name=f"result{hi - lo}")
+            nc.vector.tensor_tensor(result[:], parts[n, 0][:, lo:hi], parts[n, 1][:, lo:hi], ADD)
+            nc.sync.dma_start(out=out[n * P : (n + 1) * P, lo:hi], in_=result[:])
+
+        pick(0, 0, 0, T)
+        pick(0, 1, 0, T)
+        for n in range(1, NT):
+            pick(n, 0, 0, T)
+            store(n - 1, 0, T)
+            if n < NT - 1:
+                pick(n, 1, 0, T)
+        pick(NT - 1, 1, 0, HALF)
+        pick(NT - 1, 1, HALF, T)
+        store(NT - 1, 0, HALF)
+        store(NT - 1, HALF, T)

from contextlib import ExitStack

import concourse.mybir as mybir
from concourse.masks import make_identity

P = 128
T, E, C, K, H, N = 512, 8, 128, 512, 512, 384
NT = N // P
HALF = T // 2
FLOPS = 2 * E * C * (2 * K * H + H * N)

F32 = mybir.dt.float32
BF16 = mybir.dt.bfloat16
I32 = mybir.dt.int32
U32 = mybir.dt.uint32
U16 = mybir.dt.uint16
U8 = mybir.dt.uint8
FP8X4 = mybir.dt.float8_e4m3fn_x4
FP4X4 = mybir.dt.float4_e2m1fn_x4
MULT = mybir.AluOpType.mult
ADD = mybir.AluOpType.add
SIGMOID = mybir.ActivationFunctionType.Sigmoid

X_CHUNKS = ((0, 256), (256, 384), (384, 512))
Y_ON_VECTOR = {5: 1, 6: 1, 7: 2}


def tile_moe_pln_glu_sigmoid_kernel(
    tc, xT, w1_words, w1_scales, w3_words, w3_scales, w2_words, w2_scales, gate, offs, pos1, pos2, out
):
    nc = tc.nc
    with ExitStack() as ctx:
        keep = ctx.enter_context(tc.tile_pool(name="keep", bufs=1))
        work = ctx.enter_context(tc.tile_pool(name="work", bufs=3))
        psum = ctx.enter_context(tc.psum_pool(name="psum", bufs=2))

        offs_sb = keep.tile([P, E * C // 16], U16, name="offs_sb")
        pos1_sb = keep.tile([P, T // 16], U16, name="pos1_sb")
        pos2_sb = keep.tile([P, T // 16], U16, name="pos2_sb")

        x_raw = [keep.tile([P, 4, hi - lo], F32, name=f"x_raw{lo}") for lo, hi in X_CHUNKS]
        x_grp = [keep.tile([P, hi - lo, 4], BF16, name=f"x_grp{lo}", align_bytes=64) for lo, hi in X_CHUNKS]
        x_words = keep.tile([P, T], U32, name="x_words", align_bytes=64)
        x_bytes = keep.tile([P, T], U8, name="x_bytes", align_bytes=64)
        xv = xT.rearrange("(p j) t -> p j t", j=4)
        for i, (lo, hi) in enumerate(X_CHUNKS):
            nc.sync.dma_start(out=x_raw[i][:], in_=xv[:, :, lo:hi])
        nc.sync.dma_start(offs_sb[:], offs)

        def load_scales(plane, src):
            for r in range(4):
                nc.sync.dma_start(
                    out=plane[r:P:32, :].bitcast(I32).rearrange("q (e n) -> q e n", e=E),
                    in_=src[:, 0, r:16:4, :].rearrange("e q n -> q e n").bitcast(I32),
                )

        planes = {}
        for label, width in (("w1", H), ("w3", H), ("w2", N)):
            planes[label] = keep.tile([P, E * width], U8, name=f"{label}_sc", align_bytes=64)
        warm = keep.tile([P, 1], F32, name="warm")
        nc.vector.memset(warm[:], 0.0)
        nc.scalar.activation(warm[:], warm[:], SIGMOID)
        nc.gpsimd.memset(planes["w1"][:].bitcast(I32), 0)
        nc.vector.memset(planes["w3"][:].bitcast(I32), 0)
        nc.vector.memset(planes["w2"][:].bitcast(I32), 0)
        nc.vector.memset(x_bytes[:].bitcast(I32), 0)
        ident = keep.tile([P, P], F32, name="ident")
        make_identity(nc, ident[:])

        words_of = {}

        def load_words(label, words, lo, hi):
            width = words.shape[3]
            tile = keep.tile([P, (hi - lo) * width], U8, name=f"{label}_{lo}", align_bytes=64)
            nc.sync.dma_start(
                out=tile[:].bitcast(I32).rearrange("p (e n) -> p e n", e=hi - lo),
                in_=words[lo:hi, 0].rearrange("e p n -> p e n").bitcast(I32),
            )
            for e in range(lo, hi):
                words_of[label, e] = tile[:, (e - lo) * width : (e - lo + 1) * width]

        load_scales(planes["w1"], w1_scales)
        load_words("w1", w1_words, 0, 2)
        load_words("w3", w3_words, 0, 2)
        load_scales(planes["w3"], w3_scales)
        load_words("w1", w1_words, 2, 5)
        load_words("w3", w3_words, 2, 5)
        load_words("w2", w2_words, 0, 3)
        load_scales(planes["w2"], w2_scales)
        load_words("w1", w1_words, 5, 8)
        load_words("w3", w3_words, 5, 8)
        load_words("w2", w2_words, 3, 8)
        nc.sync.dma_start(pos1_sb[:], pos1)
        nc.sync.dma_start(pos2_sb[:], pos2)
        gates = []
        for g in range(2):
            gt = keep.tile([P, NT, T], F32, name=f"gate{g}")
            nc.sync.dma_start(out=gt[:], in_=gate[g].rearrange("(a p) t -> p a t", p=P))
            gates.append(gt)

        for i, (lo, hi) in enumerate(X_CHUNKS):
            src = x_raw[i][:].rearrange("p j t -> p t j")
            split = (hi - lo) * 11 // 16
            nc.vector.tensor_copy(out=x_grp[i][:, :split, :], in_=src[:, :split, :])
            nc.scalar.copy(out=x_grp[i][:, split:, :], in_=src[:, split:, :])
            nc.vector.quantize_mx(
                out=x_words[:, lo:hi].bitcast(FP8X4),
                scales=x_bytes[:, lo:hi],
                in_=x_grp[i][:].rearrange("p t j -> p (t j)"),
            )

        tok_words, tok_bytes = {}, {}

        def gather(lo, hi):
            width = (hi - lo) * C
            gw = keep.tile([P, width], U32, name=f"gw_{lo}", align_bytes=64)
            gb = keep.tile([P, width], U8, name=f"gb_{lo}", align_bytes=64)
            part = offs_sb[:, lo * C // 16 : hi * C // 16]
            nc.vector.tensor_copy(gw[:], x_words[:].indirect(part))
            nc.vector.tensor_copy(gb[:], x_bytes[:].indirect(part))
            for e in range(lo, hi):
                tok_words[e] = gw[:, (e - lo) * C : (e - lo + 1) * C]
                tok_bytes[e] = gb[:, (e - lo) * C : (e - lo + 1) * C]

        y_sb = [keep.tile([P, E * C], F32, name=f"y_sb{n}") for n in range(NT)]
        live = {}

        def first_layer(e):
            a_ps = psum.tile([C, H], F32, name="a_ps")
            g_ps = psum.tile([C, H], F32, name="g_ps")
            for ps, label in ((a_ps, "w1"), (g_ps, "w3")):
                nc.tensor.matmul_mx(
                    out=ps[:],
                    lhsT=tok_words[e].bitcast(FP8X4),
                    lhsT_scale=tok_bytes[e],
                    rhs=words_of[label, e].bitcast(FP4X4),
                    rhs_scale=planes[label][:, e * H : (e + 1) * H],
                    start=True,
                    stop=True,
                )
            sig = work.tile([C, H], F32, name="sig")
            nc.scalar.activation(sig[:], a_ps[:], SIGMOID)
            live[e] = (sig, g_ps)

        def product(e):
            sig, g_ps = live[e]
            h_row = work.tile([C, H], BF16, name="h_row", align_bytes=64)
            nc.vector.tensor_tensor(
                h_row[:].rearrange("c (u m d) -> c u m d", u=2, d=2),
                sig[:].rearrange("c (m u d) -> c u m d", u=2, d=2),
                g_ps[:].rearrange("c (m u d) -> c u m d", u=2, d=2),
                MULT,
            )
            live[e] = h_row

        def turn_h(e):
            h_pairs = live[e][:].bitcast(F32)
            turn = psum.tile([P, 2, C], F32, name="turn")
            for u in range(2):
                nc.tensor.transpose(turn[:, u, :], h_pairs[:, u * P : (u + 1) * P], ident[:])
            h_grp = work.tile([P, C * 4], BF16, name="h_grp", align_bytes=64)
            nc.scalar.copy(
                out=h_grp[:].bitcast(F32).rearrange("p (c u) -> p c u", u=2),
                in_=turn[:].rearrange("p u c -> p c u"),
            )
            live[e] = h_grp

        def quantise_h(e):
            h_words = work.tile([P, C], U32, name="h_words", align_bytes=64)
            h_bytes = work.tile([P, C], U8, name="h_bytes", align_bytes=64)
            nc.vector.quantize_mx(out=h_words[:].bitcast(FP8X4), scales=h_bytes[:], in_=live[e][:])
            live[e] = (h_words, h_bytes)

        def second_layer(e):
            h_words, h_bytes = live[e]
            y_ps = psum.tile([P, N], F32, name="y_ps")
            for n in range(NT):
                nc.tensor.matmul_mx(
                    out=y_ps[:, n * P : (n + 1) * P],
                    lhsT=words_of["w2", e][:, 2 * P * n : 2 * P * (n + 1)].bitcast(FP4X4),
                    lhsT_scale=planes["w2"][:, e * N + n * P : e * N + (n + 1) * P],
                    rhs=h_words[:].bitcast(FP8X4),
                    rhs_scale=h_bytes[:],
                    start=True,
                    stop=True,
                )
            live[e] = y_ps

        def keep_y(e):
            for n in range(NT):
                copy = nc.vector.tensor_copy if n < Y_ON_VECTOR.get(e, 0) else nc.scalar.copy
                copy(out=y_sb[n][:, e * C : (e + 1) * C], in_=live[e][:, n * P : (n + 1) * P])

        gathers = {-2: ((0, 1), (1, 2)), 0: ((2, 4),), 2: ((4, 6),), 4: ((6, 8),)}
        for s in range(-2, E + 3):
            for lo, hi in gathers.get(s, ()):
                gather(lo, hi)
            if 0 <= s < E:
                product(s)
            if 0 <= s - 2 < E:
                quantise_h(s - 2)
            if 0 <= s - 3 < E:
                keep_y(s - 3)
            if 0 <= s + 2 < E:
                first_layer(s + 2)
            if 0 <= s < E:
                turn_h(s)
            if 0 <= s - 2 < E:
                second_layer(s - 2)

        parts = {}

        def pick(n, which, lo, hi):
            if (n, which) not in parts:
                parts[n, which] = keep.tile([P, T], F32, name=f"part{n}{which}")
            pos = (pos1_sb, pos2_sb)[which]
            nc.vector.tensor_tensor(
                parts[n, which][:, lo:hi], y_sb[n][:].indirect(pos[:, lo // 16 : hi // 16]), gates[which][:, n, lo:hi], MULT
            )

        def store(n, lo, hi):
            result = work.tile([P, hi - lo], F32, name=f"result{hi - lo}")
            nc.vector.tensor_tensor(result[:], parts[n, 0][:, lo:hi], parts[n, 1][:, lo:hi], ADD)
            nc.sync.dma_start(out=out[n * P : (n + 1) * P, lo:hi], in_=result[:])

        pick(0, 0, 0, T)
        pick(0, 1, 0, T)
        for n in range(1, NT):
            pick(n, 0, 0, T)
            store(n - 1, 0, T)
            if n < NT - 1:
                pick(n, 1, 0, T)
        pick(NT - 1, 1, 0, HALF)
        pick(NT - 1, 1, HALF, T)
        store(NT - 1, 0, HALF)
        store(NT - 1, HALF, T)
